import numpy as np
import ml_dtypes


def mxq(x, axis, fmt="e4m3"):
    dtype, down = {"e4m3": (ml_dtypes.float8_e4m3fn, 7), "e5m2": (ml_dtypes.float8_e5m2, 14)}[fmt]
    v = np.moveaxis(np.asarray(x, np.float32).astype(ml_dtypes.bfloat16).astype(np.float64), axis, -1)
    blocks = v.reshape(v.shape[:-1] + (-1, 32))
    amax = np.abs(blocks).max(-1, keepdims=True)
    byte = np.maximum(np.where(amax > 0, np.frexp(amax)[1] - 1 + 127, 0) - down, 1)
    scale = np.exp2(byte - 127.0)
    codes = (blocks / scale).astype(np.float32).astype(dtype).astype(np.float64)
    return np.moveaxis((codes * scale).reshape(v.shape), -1, axis)


WIDE = False


def mx_kscale(k):
    if not WIDE:
        return np.ones(k)
    levels = np.array([10, -10, 5, -5, 0])
    if k % 512:
        return np.exp2(np.random.permutation(np.resize(levels, k // 32))).repeat(32)
    a = np.empty((k // 512, 16))
    for p in range(k // 512):
        a[p, :8] = np.random.permutation(np.resize(levels, 8))
        for g in range(8):
            far = levels[np.abs(levels - a[p, g]) >= 10]
            a[p, g + 8] = far[np.random.randint(len(far))]
    return np.exp2(a.ravel()).repeat(32)


def f64(x):
    return np.asarray(x).astype(np.float64)


def striped(idx):
    return np.tile(np.asarray(idx).reshape(-1, 16).T, (8, 1)).astype(np.uint16)


def unstriped(offs):
    return offs[:16].T.reshape(-1).astype(np.int64)


E2M1 = np.array([0.0, 0.5, 1.0, 1.5, 2.0, 3.0, 4.0, 6.0, -0.0, -0.5, -1.0, -1.5, -2.0, -3.0, -4.0, -6.0])


def pack_weight(w, fmt):
    k, n = w.shape
    w = f64(np.asarray(w, np.float32).astype(ml_dtypes.bfloat16)).reshape(k // 32, 32, n)
    amax = np.abs(w).max(1)
    if fmt == "e4m3":
        byte = np.frexp(amax)[1] - 1 + 127 - 7
    else:
        mant, ex = np.frexp(amax / 6.0)
        byte = np.where(mant > 0.5, ex, ex - 1) + 127
    byte = np.clip(np.where(amax > 0, byte, 1), 1, 254)
    scaled = (w * np.exp2(127.0 - byte)[:, None, :]).reshape(k, n).astype(np.float32)
    by_word = np.ascontiguousarray(scaled.reshape(k // 512, 128, 4, n).transpose(0, 1, 3, 2))
    if fmt == "e4m3":
        words = by_word.astype(ml_dtypes.float8_e4m3fn).view(np.uint8)
    else:
        c = by_word.astype(ml_dtypes.float4_e2m1fn).view(np.uint8) & 0xF
        words = (c[..., 0::2] | (c[..., 1::2] << 4)).reshape(k // 512, 128, 2 * n)
    return np.ascontiguousarray(words), np.ascontiguousarray(byte.astype(np.uint8).reshape(k // 512, 16, n))


def unpack_weight(words, scales, fmt):
    g, _, n = scales.shape
    words = np.ascontiguousarray(words).reshape(g, 128, n, -1)
    if fmt == "e4m3":
        vals = words.view(ml_dtypes.float8_e4m3fn).astype(np.float64)
    else:
        nib = np.empty((g, 128, n, 4), np.uint8)
        nib[..., 0::2] = words & 0xF
        nib[..., 1::2] = words >> 4
        vals = E2M1[nib]
    vals = vals * np.repeat(np.exp2(scales.astype(np.float64) - 127.0), 8, axis=1)[..., None]
    return vals.transpose(0, 1, 3, 2).reshape(g * 512, n)


def e4m3fn_bytes(y):
    return np.clip(np.asarray(y, np.float64), -448.0, 448.0).astype(np.float32).astype(ml_dtypes.float8_e4m3fn).view(np.uint8)


def e4m3fn_values(b):
    return np.asarray(b, np.uint8).view(ml_dtypes.float8_e4m3fn).astype(np.float64)


K, T, J, R, V, D, N = 512, 1024, 256, 512, 1024, 2048, 256


def setup_inputs():
    n = np.random.standard_normal
    idx = np.random.permutation(V)[:R]
    idx2 = np.random.permutation(T)[:J]
    idx3 = np.random.permutation(D)[:J]
    fk = mx_kscale(K)
    fr = mx_kscale(R)
    xtp = pack_weight(n((K, T)) / fk[:, None], "e2m1")
    wtp = pack_weight(n((K, V)) * 1 / np.sqrt(K) * fk[:, None], "e4m3")
    wbp = pack_weight(n((R, N)) * 1 / np.sqrt(R) / fr[:, None], "e2m1")
    return {
        "xt_words": xtp[0],
        "xt_scales": xtp[1],
        "wt_words": wtp[0],
        "wt_scales": wtp[1],
        "ca": e4m3fn_bytes(60.0 * n((R, D))),
        "st": (np.random.uniform(0.004, 0.012, (R, 1)) * fr[:, None]).astype(np.float32),
        "wb_words": wbp[0],
        "wb_scales": wbp[1],
        "offs": striped(idx),
        "offs2": striped(idx2),
        "offs3": striped(idx3),
    }


def reference(xt_words, xt_scales, wt_words, wt_scales, ca, st, wb_words, wb_scales, offs, offs2, offs3):
    idx = unstriped(offs)
    idx2 = unstriped(offs2)
    idx3 = unstriped(offs3)
    xtu = unpack_weight(xt_words, xt_scales, "e2m1")
    wtu = unpack_weight(wt_words, wt_scales, "e4m3")
    wbu = unpack_weight(wb_words, wb_scales, "e2m1")
    wtidxg = wtu[:, idx]
    xtidx2g = xtu[:, idx2]
    a = wtidxg.T @ xtidx2g
    g1 = e4m3fn_values(ca)[:, idx3] * f64(st)
    g2 = np.pad(g1, ((0, 0), (1, 0)))[:, :J]
    hid = a * (g1 - g2)
    hidq = mxq(hid, 0, "e4m3")
    p = wbu.T @ hidq
    return p

@@ -1,0 +1,141 @@
+from contextlib import ExitStack
+
+import concourse.mybir as mybir
+
+K, T, J, R, V, D, N = 512, 1024, 256, 512, 1024, 2048, 256
+FLOPS = 2 * K * R * J + 2 * R * N * J
+
+F32 = mybir.dt.float32
+BF16 = mybir.dt.bfloat16
+I32 = mybir.dt.int32
+U32 = mybir.dt.uint32
+U16 = mybir.dt.uint16
+U8 = mybir.dt.uint8
+FP8 = mybir.dt.float8_e4m3fn
+FP8X4 = mybir.dt.float8_e4m3fn_x4
+FP4X4 = mybir.dt.float4_e2m1fn_x4
+MULT = mybir.AluOpType.mult
+SUB = mybir.AluOpType.subtract
+COPY = mybir.ActivationFunctionType.Copy
+
+P = 128
+PACK = 4
+HALF = J // 2
+LEAD = 4
+
+
+def load_scale_rows(queue, plane, rows):
+    for q in range(4):
+        queue.dma_start(plane[32 * q : 32 * q + 4, :].bitcast(I32), rows[4 * q : 4 * q + 4, :].bitcast(I32))
+
+
+def tile_list_increments_kernel(
+    tc, xt_words, xt_scales, wt_words, wt_scales, ca, st, wb_words, wb_scales, offs, offs2, offs3, out
+):
+    nc = tc.nc
+    with ExitStack() as ctx:
+        pool = ctx.enter_context(tc.tile_pool(name="sb", bufs=1))
+        psum = ctx.enter_context(tc.psum_pool(name="ps", bufs=1))
+
+        feat_list = pool.tile([P, R // 16], U16, name="feat_list")
+        tok_list = pool.tile([P, J // 16], U16, name="tok_list")
+        frame_list = pool.tile([P, J // 16], U16, name="frame_list")
+        xt_w = pool.tile([P, T], U16, name="xt_w", align_bytes=64)
+        xt_s = pool.tile([P, T], U8, name="xt_s", align_bytes=64)
+        wt_w = pool.tile([P, V], U32, name="wt_w", align_bytes=64)
+        wt_s = pool.tile([P, V], U8, name="wt_s", align_bytes=64)
+        wb_w = pool.tile([P, N], U16, name="wb_w", align_bytes=64)
+        wb_s = pool.tile([P, N], U8, name="wb_s", align_bytes=64)
+        steps = pool.tile([P, PACK], F32, name="steps")
+        frames = [pool.tile([P, D], U8, name="frames%d" % t, align_bytes=64) for t in range(PACK)]
+        g1 = pool.tile([P, PACK, LEAD + J], F32, name="g1", align_bytes=64)
+
+        nc.vector.memset(xt_s[:].bitcast(I32), 0)
+        nc.vector.memset(wt_s[:].bitcast(I32), 0)
+        nc.vector.memset(wb_s[:].bitcast(I32), 0)
+        nc.vector.memset(g1[:, :, LEAD - 1 : LEAD], 0.0)
+
+        ca_rows = ca.rearrange("(p t) d -> t p d", t=PACK)
+        nc.sync.dma_start(tok_list[:], offs2)
+        nc.sync.dma_start(xt_w[:].bitcast(I32), xt_words[0].bitcast(I32))
+        load_scale_rows(nc.scalar, xt_s, xt_scales[0])
+        nc.sync.dma_start(feat_list[:], offs)
+        nc.sync.dma_start(wt_w[:].bitcast(I32), wt_words[0].rearrange("p n t -> p (n t)").bitcast(I32))
+        nc.sync.dma_start(frame_list[:], offs3)
+        nc.sync.dma_start(frames[0][:], ca_rows[0])
+        load_scale_rows(nc.scalar, wt_s, wt_scales[0])
+        for t in range(1, PACK):
+            nc.sync.dma_start(frames[t][:], ca_rows[t])
+        nc.sync.dma_start(steps[:], st.rearrange("(p t) o -> p (t o)", t=PACK))
+        nc.sync.dma_start(wb_w[:].bitcast(I32), wb_words[0].bitcast(I32))
+        load_scale_rows(nc.sync, wb_s, wb_scales[0])
+
+        xg_w = pool.tile([P, J], U16, name="xg_w", align_bytes=64)
+        xg_s = pool.tile([P, J], U8, name="xg_s", align_bytes=64)
+        wg_w = pool.tile([P, R], U32, name="wg_w", align_bytes=64)
+        wg_s = pool.tile([P, R], U8, name="wg_s", align_bytes=64)
+        nc.vector.tensor_copy(xg_w[:], xt_w[:].indirect(tok_list[:]))
+        nc.vector.tensor_copy(xg_s[:], xt_s[:].indirect(tok_list[:]))
+        nc.vector.tensor_copy(wg_w[:].rearrange("p (t m) -> p m t", t=PACK), wt_w[:].indirect(feat_list[:]))
+        nc.vector.tensor_copy(wg_s[:].rearrange("p (t m) -> p m t", t=PACK), wt_s[:].indirect(feat_list[:]))
+
+        a_banks = [psum.tile([P, PACK, HALF], F32, name="a_bank%d" % h) for h in range(2)]
+        for h in range(2):
+            cols = slice(h * HALF, (h + 1) * HALF)
+            for t in range(PACK):
+                feats = slice(t * P, (t + 1) * P)
+                nc.tensor.matmul_mx(
+                    out=a_banks[h][:, t, :],
+                    lhsT=wg_w[:, feats].bitcast(FP8X4),
+                    lhsT_scale=wg_s[:, feats],
+                    rhs=xg_w[:, cols].bitcast(FP4X4),
+                    rhs_scale=xg_s[:, cols],
+                    start=True,
+                    stop=True,
+                )
+
+        picked = [pool.tile([P, J], U8, name="picked%d" % t, align_bytes=64) for t in range(PACK)]
+        for t in range(PACK):
+            nc.vector.tensor_copy(picked[t][:], frames[t][:].indirect(frame_list[:]))
+            nc.scalar.activation(g1[:, t, LEAD:], picked[t][:].bitcast(FP8), COPY, scale=steps[:, t : t + 1])
+
+        incr = pool.tile([P, PACK, J], F32, name="incr", align_bytes=64)
+        for u in range(2):
+            rows = slice(2 * u, 2 * u + 2)
+            nc.vector.tensor_tensor(incr[:, rows, :], g1[:, rows, LEAD:], g1[:, rows, LEAD - 1 : LEAD - 1 + J], SUB)
+
+        hid = [pool.tile([P, HALF * PACK], BF16, name="hid%d" % h, align_bytes=64) for h in range(2)]
+        hid_w = [pool.tile([P, HALF], U32, name="hid_w%d" % h, align_bytes=64) for h in range(2)]
+        hid_s = [pool.tile([P, HALF], U8, name="hid_s%d" % h, align_bytes=64) for h in range(2)]
+        for h in range(2):
+            cols = slice(h * HALF, (h + 1) * HALF)
+            nc.vector.tensor_tensor(
+                hid[h][:].rearrange("p (c i t) -> p c t i", i=4, t=PACK),
+                a_banks[h][:].rearrange("p t (c i) -> p c t i", i=4),
+                incr[:, :, cols].rearrange("p t (c i) -> p c t i", i=4),
+                MULT,
+            )
+        for h in range(2):
+            nc.vector.quantize_mx(out=hid_w[h][:].bitcast(FP8X4), scales=hid_s[h][:], in_=hid[h][:])
+
+        for h in range(2):
+            cols = slice(h * HALF, (h + 1) * HALF)
+            for b in range(N // P):
+                outs = slice(b * P, (b + 1) * P)
+                acc = psum.tile([P, HALF], F32, name="acc%d%d" % (h, b))
+                nc.tensor.matmul_mx(
+                    out=acc[:],
+                    lhsT=wb_w[:, outs].bitcast(FP4X4),
+                    lhsT_scale=wb_s[:, outs],
+                    rhs=hid_w[h][:].bitcast(FP8X4),
+                    rhs_scale=hid_s[h][:],
+                    start=True,
+                    stop=True,
+                )
+                res = pool.tile([P, HALF], F32, name="res%d%d" % (h, b))
+                if h == 1 and b == 1:
+                    nc.vector.tensor_copy(res[:], acc[:])
+                    nc.sync.dma_start(out[outs, cols], res[:])
+                else:
+                    nc.scalar.copy(res[:], acc[:])
+                    (nc.scalar if h == 1 else nc.sync).dma_start(out[outs, cols], res[:])

@@ -40,7 +40,7 @@ def tile_list_increments_kernel(
         feat_list = pool.tile([P, R // 16], U16, name="feat_list")
         tok_list = pool.tile([P, J // 16], U16, name="tok_list")
         frame_list = pool.tile([P, J // 16], U16, name="frame_list")
-        xt_w = pool.tile([P, T], U16, name="xt_w", align_bytes=64)
+        xt_w = pool.tile([P, T], U16, name="xt_w", tag="tokens_then_incr", align_bytes=64)
         xt_s = pool.tile([P, T], U8, name="xt_s", align_bytes=64)
         wt_w = pool.tile([P, V], U32, name="wt_w", align_bytes=64)
         wt_s = pool.tile([P, V], U8, name="wt_s", align_bytes=64)
@@ -50,23 +50,25 @@ def tile_list_increments_kernel(
         frames = [pool.tile([P, D], U8, name="frames%d" % t, align_bytes=64) for t in range(PACK)]
         g1 = pool.tile([P, PACK, LEAD + J], F32, name="g1", align_bytes=64)
 
-        nc.vector.memset(xt_s[:].bitcast(I32), 0)
         nc.vector.memset(wt_s[:].bitcast(I32), 0)
+        nc.vector.memset(xt_s[:].bitcast(I32), 0)
+        zeros = pool.tile([P, PACK, LEAD], F32, name="zeros")
+        nc.vector.memset(zeros[:], 0.0)
         nc.vector.memset(wb_s[:].bitcast(I32), 0)
-        nc.vector.memset(g1[:, :, LEAD - 1 : LEAD], 0.0)
+        nc.scalar.activation(g1[:, :, :LEAD], zeros[:], COPY)
 
         ca_rows = ca.rearrange("(p t) d -> t p d", t=PACK)
-        nc.sync.dma_start(tok_list[:], offs2)
-        nc.sync.dma_start(xt_w[:].bitcast(I32), xt_words[0].bitcast(I32))
-        load_scale_rows(nc.scalar, xt_s, xt_scales[0])
-        nc.sync.dma_start(feat_list[:], offs)
-        nc.sync.dma_start(wt_w[:].bitcast(I32), wt_words[0].rearrange("p n t -> p (n t)").bitcast(I32))
+        nc.gpsimd.dma_start(steps[:], st.rearrange("(p t) o -> p (t o)", t=PACK))
         nc.sync.dma_start(frame_list[:], offs3)
         nc.sync.dma_start(frames[0][:], ca_rows[0])
-        load_scale_rows(nc.scalar, wt_s, wt_scales[0])
+        nc.sync.dma_start(feat_list[:], offs)
+        load_scale_rows(nc.sync, wt_s, wt_scales[0])
+        nc.sync.dma_start(wt_w[:].bitcast(I32), wt_words[0].rearrange("p n t -> p (n t)").bitcast(I32))
         for t in range(1, PACK):
             nc.sync.dma_start(frames[t][:], ca_rows[t])
-        nc.sync.dma_start(steps[:], st.rearrange("(p t) o -> p (t o)", t=PACK))
+        load_scale_rows(nc.sync, xt_s, xt_scales[0])
+        nc.sync.dma_start(xt_w[:].bitcast(I32), xt_words[0].bitcast(I32))
+        nc.sync.dma_start(tok_list[:], offs2)
         nc.sync.dma_start(wb_w[:].bitcast(I32), wb_words[0].bitcast(I32))
         load_scale_rows(nc.sync, wb_s, wb_scales[0])
 
@@ -99,20 +101,21 @@ def tile_list_increments_kernel(
             nc.vector.tensor_copy(picked[t][:], frames[t][:].indirect(frame_list[:]))
             nc.scalar.activation(g1[:, t, LEAD:], picked[t][:].bitcast(FP8), COPY, scale=steps[:, t : t + 1])
 
-        incr = pool.tile([P, PACK, J], F32, name="incr", align_bytes=64)
-        for u in range(2):
-            rows = slice(2 * u, 2 * u + 2)
-            nc.vector.tensor_tensor(incr[:, rows, :], g1[:, rows, LEAD:], g1[:, rows, LEAD - 1 : LEAD - 1 + J], SUB)
+        incr = pool.tile([P, 2, PACK, HALF], F32, name="incr", tag="tokens_then_incr", align_bytes=64)
+        for h in range(2):
+            first = LEAD + h * HALF
+            nc.vector.tensor_tensor(
+                incr[:, h], g1[:, :, first : first + HALF], g1[:, :, first - 1 : first - 1 + HALF], SUB
+            )
 
         hid = [pool.tile([P, HALF * PACK], BF16, name="hid%d" % h, align_bytes=64) for h in range(2)]
         hid_w = [pool.tile([P, HALF], U32, name="hid_w%d" % h, align_bytes=64) for h in range(2)]
         hid_s = [pool.tile([P, HALF], U8, name="hid_s%d" % h, align_bytes=64) for h in range(2)]
         for h in range(2):
-            cols = slice(h * HALF, (h + 1) * HALF)
             nc.vector.tensor_tensor(
                 hid[h][:].rearrange("p (c i t) -> p c t i", i=4, t=PACK),
                 a_banks[h][:].rearrange("p t (c i) -> p c t i", i=4),
-                incr[:, :, cols].rearrange("p t (c i) -> p c t i", i=4),
+                incr[:, h].rearrange("p t (c i) -> p c t i", i=4),
                 MULT,
             )
         for h in range(2):
@@ -133,7 +136,7 @@ def tile_list_increments_kernel(
                     stop=True,
                 )
                 res = pool.tile([P, HALF], F32, name="res%d%d" % (h, b))
-                if h == 1 and b == 1:
+                if b == 1:
                     nc.vector.tensor_copy(res[:], acc[:])
                     nc.sync.dma_start(out[outs, cols], res[:])
                 else:

@@ -40,7 +40,7 @@ def tile_list_increments_kernel(
         feat_list = pool.tile([P, R // 16], U16, name="feat_list")
         tok_list = pool.tile([P, J // 16], U16, name="tok_list")
         frame_list = pool.tile([P, J // 16], U16, name="frame_list")
-        xt_w = pool.tile([P, T], U16, name="xt_w", tag="tokens_then_incr", align_bytes=64)
+        xt_w = pool.tile([P, T], U16, name="xt_w", align_bytes=64)
         xt_s = pool.tile([P, T], U8, name="xt_s", align_bytes=64)
         wt_w = pool.tile([P, V], U32, name="wt_w", align_bytes=64)
         wt_s = pool.tile([P, V], U8, name="wt_s", align_bytes=64)
@@ -72,41 +72,44 @@ def tile_list_increments_kernel(
         nc.sync.dma_start(wb_w[:].bitcast(I32), wb_words[0].bitcast(I32))
         load_scale_rows(nc.sync, wb_s, wb_scales[0])
 
-        xg_w = pool.tile([P, J], U16, name="xg_w", align_bytes=64)
-        xg_s = pool.tile([P, J], U8, name="xg_s", align_bytes=64)
+        xg_w = [pool.tile([P, HALF], U16, name="xg_w%d" % h, align_bytes=64) for h in range(2)]
+        xg_s = [pool.tile([P, HALF], U8, name="xg_s%d" % h, align_bytes=64) for h in range(2)]
         wg_w = pool.tile([P, R], U32, name="wg_w", align_bytes=64)
         wg_s = pool.tile([P, R], U8, name="wg_s", align_bytes=64)
-        nc.vector.tensor_copy(xg_w[:], xt_w[:].indirect(tok_list[:]))
-        nc.vector.tensor_copy(xg_s[:], xt_s[:].indirect(tok_list[:]))
+        for h in range(2):
+            entries = tok_list[:, h * HALF // 16 : (h + 1) * HALF // 16]
+            nc.vector.tensor_copy(xg_w[h][:], xt_w[:].indirect(entries))
+            nc.vector.tensor_copy(xg_s[h][:], xt_s[:].indirect(entries))
         nc.vector.tensor_copy(wg_w[:].rearrange("p (t m) -> p m t", t=PACK), wt_w[:].indirect(feat_list[:]))
         nc.vector.tensor_copy(wg_s[:].rearrange("p (t m) -> p m t", t=PACK), wt_s[:].indirect(feat_list[:]))
 
         a_banks = [psum.tile([P, PACK, HALF], F32, name="a_bank%d" % h) for h in range(2)]
         for h in range(2):
-            cols = slice(h * HALF, (h + 1) * HALF)
             for t in range(PACK):
                 feats = slice(t * P, (t + 1) * P)
                 nc.tensor.matmul_mx(
                     out=a_banks[h][:, t, :],
                     lhsT=wg_w[:, feats].bitcast(FP8X4),
                     lhsT_scale=wg_s[:, feats],
-                    rhs=xg_w[:, cols].bitcast(FP4X4),
-                    rhs_scale=xg_s[:, cols],
+                    rhs=xg_w[h][:].bitcast(FP4X4),
+                    rhs_scale=xg_s[h][:],
                     start=True,
                     stop=True,
                 )
 
         picked = [pool.tile([P, J], U8, name="picked%d" % t, align_bytes=64) for t in range(PACK)]
+        incr = pool.tile([P, PACK, J], F32, name="incr", align_bytes=64)
         for t in range(PACK):
             nc.vector.tensor_copy(picked[t][:], frames[t][:].indirect(frame_list[:]))
             nc.scalar.activation(g1[:, t, LEAD:], picked[t][:].bitcast(FP8), COPY, scale=steps[:, t : t + 1])
-
-        incr = pool.tile([P, 2, PACK, HALF], F32, name="incr", tag="tokens_then_incr", align_bytes=64)
-        for h in range(2):
-            first = LEAD + h * HALF
-            nc.vector.tensor_tensor(
-                incr[:, h], g1[:, :, first : first + HALF], g1[:, :, first - 1 : first - 1 + HALF], SUB
-            )
+            width = HALF if t == PACK - 1 else J
+            for c in range(0, J, width):
+                nc.gpsimd.tensor_tensor(
+                    incr[:, t, c : c + width],
+                    g1[:, t, LEAD + c : LEAD + c + width],
+                    g1[:, t, LEAD + c - 1 : LEAD + c - 1 + width],
+                    SUB,
+                )
 
         hid = [pool.tile([P, HALF * PACK], BF16, name="hid%d" % h, align_bytes=64) for h in range(2)]
         hid_w = [pool.tile([P, HALF], U32, name="hid_w%d" % h, align_bytes=64) for h in range(2)]
@@ -115,7 +118,7 @@ def tile_list_increments_kernel(
             nc.vector.tensor_tensor(
                 hid[h][:].rearrange("p (c i t) -> p c t i", i=4, t=PACK),
                 a_banks[h][:].rearrange("p t (c i) -> p c t i", i=4),
-                incr[:, h].rearrange("p t (c i) -> p c t i", i=4),
+                incr[:, :, h * HALF : (h + 1) * HALF].rearrange("p t (c i) -> p c t i", i=4),
                 MULT,
             )
         for h in range(2):

from contextlib import ExitStack

import concourse.mybir as mybir

K, T, J, R, V, D, N = 512, 1024, 256, 512, 1024, 2048, 256
FLOPS = 2 * K * R * J + 2 * R * N * J

F32 = mybir.dt.float32
BF16 = mybir.dt.bfloat16
I32 = mybir.dt.int32
U32 = mybir.dt.uint32
U16 = mybir.dt.uint16
U8 = mybir.dt.uint8
FP8 = mybir.dt.float8_e4m3fn
FP8X4 = mybir.dt.float8_e4m3fn_x4
FP4X4 = mybir.dt.float4_e2m1fn_x4
MULT = mybir.AluOpType.mult
SUB = mybir.AluOpType.subtract
COPY = mybir.ActivationFunctionType.Copy

P = 128
PACK = 4
HALF = J // 2
LEAD = 4


def load_scale_rows(queue, plane, rows):
    for q in range(4):
        queue.dma_start(plane[32 * q : 32 * q + 4, :].bitcast(I32), rows[4 * q : 4 * q + 4, :].bitcast(I32))


def tile_list_increments_kernel(
    tc, xt_words, xt_scales, wt_words, wt_scales, ca, st, wb_words, wb_scales, offs, offs2, offs3, out
):
    nc = tc.nc
    with ExitStack() as ctx:
        pool = ctx.enter_context(tc.tile_pool(name="sb", bufs=1))
        psum = ctx.enter_context(tc.psum_pool(name="ps", bufs=1))

        feat_list = pool.tile([P, R // 16], U16, name="feat_list")
        tok_list = pool.tile([P, J // 16], U16, name="tok_list")
        frame_list = pool.tile([P, J // 16], U16, name="frame_list")
        xt_w = pool.tile([P, T], U16, name="xt_w", align_bytes=64)
        xt_s = pool.tile([P, T], U8, name="xt_s", align_bytes=64)
        wt_w = pool.tile([P, V], U32, name="wt_w", align_bytes=64)
        wt_s = pool.tile([P, V], U8, name="wt_s", align_bytes=64)
        wb_w = pool.tile([P, N], U16, name="wb_w", align_bytes=64)
        wb_s = pool.tile([P, N], U8, name="wb_s", align_bytes=64)
        steps = pool.tile([P, PACK], F32, name="steps")
        frames = [pool.tile([P, D], U8, name="frames%d" % t, align_bytes=64) for t in range(PACK)]
        g1 = pool.tile([P, PACK, LEAD + J], F32, name="g1", align_bytes=64)

        nc.vector.memset(wt_s[:].bitcast(I32), 0)
        nc.vector.memset(xt_s[:].bitcast(I32), 0)
        zeros = pool.tile([P, PACK, LEAD], F32, name="zeros")
        nc.vector.memset(zeros[:], 0.0)
        nc.vector.memset(wb_s[:].bitcast(I32), 0)
        nc.scalar.activation(g1[:, :, :LEAD], zeros[:], COPY)

        ca_rows = ca.rearrange("(p t) d -> t p d", t=PACK)
        nc.gpsimd.dma_start(steps[:], st.rearrange("(p t) o -> p (t o)", t=PACK))
        nc.sync.dma_start(frame_list[:], offs3)
        nc.sync.dma_start(frames[0][:], ca_rows[0])
        nc.sync.dma_start(feat_list[:], offs)
        load_scale_rows(nc.sync, wt_s, wt_scales[0])
        nc.sync.dma_start(wt_w[:].bitcast(I32), wt_words[0].rearrange("p n t -> p (n t)").bitcast(I32))
        for t in range(1, PACK):
            nc.sync.dma_start(frames[t][:], ca_rows[t])
        load_scale_rows(nc.sync, xt_s, xt_scales[0])
        nc.sync.dma_start(xt_w[:].bitcast(I32), xt_words[0].bitcast(I32))
        nc.sync.dma_start(tok_list[:], offs2)
        nc.sync.dma_start(wb_w[:].bitcast(I32), wb_words[0].bitcast(I32))
        load_scale_rows(nc.sync, wb_s, wb_scales[0])

        xg_w = [pool.tile([P, HALF], U16, name="xg_w%d" % h, align_bytes=64) for h in range(2)]
        xg_s = [pool.tile([P, HALF], U8, name="xg_s%d" % h, align_bytes=64) for h in range(2)]
        wg_w = pool.tile([P, R], U32, name="wg_w", align_bytes=64)
        wg_s = pool.tile([P, R], U8, name="wg_s", align_bytes=64)
        for h in range(2):
            entries = tok_list[:, h * HALF // 16 : (h + 1) * HALF // 16]
            nc.vector.tensor_copy(xg_w[h][:], xt_w[:].indirect(entries))
            nc.vector.tensor_copy(xg_s[h][:], xt_s[:].indirect(entries))
        nc.vector.tensor_copy(wg_w[:].rearrange("p (t m) -> p m t", t=PACK), wt_w[:].indirect(feat_list[:]))
        nc.vector.tensor_copy(wg_s[:].rearrange("p (t m) -> p m t", t=PACK), wt_s[:].indirect(feat_list[:]))

        a_banks = [psum.tile([P, PACK, HALF], F32, name="a_bank%d" % h) for h in range(2)]
        for h in range(2):
            for t in range(PACK):
                feats = slice(t * P, (t + 1) * P)
                nc.tensor.matmul_mx(
                    out=a_banks[h][:, t, :],
                    lhsT=wg_w[:, feats].bitcast(FP8X4),
                    lhsT_scale=wg_s[:, feats],
                    rhs=xg_w[h][:].bitcast(FP4X4),
                    rhs_scale=xg_s[h][:],
                    start=True,
                    stop=True,
                )

        picked = [pool.tile([P, J], U8, name="picked%d" % t, align_bytes=64) for t in range(PACK)]
        incr = pool.tile([P, PACK, J], F32, name="incr", align_bytes=64)
        for t in range(PACK):
            nc.vector.tensor_copy(picked[t][:], frames[t][:].indirect(frame_list[:]))
            nc.scalar.activation(g1[:, t, LEAD:], picked[t][:].bitcast(FP8), COPY, scale=steps[:, t : t + 1])
            width = HALF if t == PACK - 1 else J
            for c in range(0, J, width):
                nc.gpsimd.tensor_tensor(
                    incr[:, t, c : c + width],
                    g1[:, t, LEAD + c : LEAD + c + width],
                    g1[:, t, LEAD + c - 1 : LEAD + c - 1 + width],
                    SUB,
                )

        hid = [pool.tile([P, HALF * PACK], BF16, name="hid%d" % h, align_bytes=64) for h in range(2)]
        hid_w = [pool.tile([P, HALF], U32, name="hid_w%d" % h, align_bytes=64) for h in range(2)]
        hid_s = [pool.tile([P, HALF], U8, name="hid_s%d" % h, align_bytes=64) for h in range(2)]
        for h in range(2):
            nc.vector.tensor_tensor(
                hid[h][:].rearrange("p (c i t) -> p c t i", i=4, t=PACK),
                a_banks[h][:].rearrange("p t (c i) -> p c t i", i=4),
                incr[:, :, h * HALF : (h + 1) * HALF].rearrange("p t (c i) -> p c t i", i=4),
                MULT,
            )
        for h in range(2):
            nc.vector.quantize_mx(out=hid_w[h][:].bitcast(FP8X4), scales=hid_s[h][:], in_=hid[h][:])

        for h in range(2):
            cols = slice(h * HALF, (h + 1) * HALF)
            for b in range(N // P):
                outs = slice(b * P, (b + 1) * P)
                acc = psum.tile([P, HALF], F32, name="acc%d%d" % (h, b))
                nc.tensor.matmul_mx(
                    out=acc[:],
                    lhsT=wb_w[:, outs].bitcast(FP4X4),
                    lhsT_scale=wb_s[:, outs],
                    rhs=hid_w[h][:].bitcast(FP8X4),
                    rhs_scale=hid_s[h][:],
                    start=True,
                    stop=True,
                )
                res = pool.tile([P, HALF], F32, name="res%d%d" % (h, b))
                if b == 1:
                    nc.vector.tensor_copy(res[:], acc[:])
                    nc.sync.dma_start(out[outs, cols], res[:])
                else:
                    nc.scalar.copy(res[:], acc[:])
                    (nc.scalar if h == 1 else nc.sync).dma_start(out[outs, cols], res[:])
